import numpy as np
import ml_dtypes


def mxq(x, axis, fmt="e4m3"):
    dtype, down = {"e4m3": (ml_dtypes.float8_e4m3fn, 7), "e5m2": (ml_dtypes.float8_e5m2, 14)}[fmt]
    v = np.moveaxis(np.asarray(x, np.float32).astype(ml_dtypes.bfloat16).astype(np.float64), axis, -1)
    blocks = v.reshape(v.shape[:-1] + (-1, 32))
    amax = np.abs(blocks).max(-1, keepdims=True)
    byte = np.maximum(np.where(amax > 0, np.frexp(amax)[1] - 1 + 127, 0) - down, 1)
    scale = np.exp2(byte - 127.0)
    codes = (blocks / scale).astype(np.float32).astype(dtype).astype(np.float64)
    return np.moveaxis((codes * scale).reshape(v.shape), -1, axis)


WIDE = False


def mx_kscale(k):
    if not WIDE:
        return np.ones(k)
    levels = np.array([10, -10, 5, -5, 0])
    if k % 512:
        return np.exp2(np.random.permutation(np.resize(levels, k // 32))).repeat(32)
    a = np.empty((k // 512, 16))
    for p in range(k // 512):
        a[p, :8] = np.random.permutation(np.resize(levels, 8))
        for g in range(8):
            far = levels[np.abs(levels - a[p, g]) >= 10]
            a[p, g + 8] = far[np.random.randint(len(far))]
    return np.exp2(a.ravel()).repeat(32)


BF16 = ml_dtypes.bfloat16


def bf(x):
    return np.asarray(x, np.float32).astype(BF16)


def f64(x):
    return np.asarray(x).astype(np.float64)


E2M1 = np.array([0.0, 0.5, 1.0, 1.5, 2.0, 3.0, 4.0, 6.0, -0.0, -0.5, -1.0, -1.5, -2.0, -3.0, -4.0, -6.0])


def pack_weight(w, fmt):
    k, n = w.shape
    w = f64(bf(w)).reshape(k // 32, 32, n)
    amax = np.abs(w).max(1)
    if fmt == "e4m3":
        byte = np.frexp(amax)[1] - 1 + 127 - 7
    else:
        mant, ex = np.frexp(amax / 6.0)
        byte = np.where(mant > 0.5, ex, ex - 1) + 127
    byte = np.clip(np.where(amax > 0, byte, 1), 1, 254)
    scaled = (w * np.exp2(127.0 - byte)[:, None, :]).reshape(k, n).astype(np.float32)
    by_word = np.ascontiguousarray(scaled.reshape(k // 512, 128, 4, n).transpose(0, 1, 3, 2))
    if fmt == "e4m3":
        words = by_word.astype(ml_dtypes.float8_e4m3fn).view(np.uint8)
    else:
        c = by_word.astype(ml_dtypes.float4_e2m1fn).view(np.uint8) & 0xF
        words = c[..., 0::2] | (c[..., 1::2] << 4)
    return np.ascontiguousarray(words), np.ascontiguousarray(byte.astype(np.uint8).reshape(k // 512, 16, n))


def unpack_weight(words, scales, fmt):
    g, p, n, _ = words.shape
    if fmt == "e4m3":
        vals = np.ascontiguousarray(words).view(ml_dtypes.float8_e4m3fn).astype(np.float64)
    else:
        nib = np.empty((g, p, n, 4), np.uint8)
        nib[..., 0::2] = words & 0xF
        nib[..., 1::2] = words >> 4
        vals = E2M1[nib]
    vals = vals * np.repeat(np.exp2(scales.astype(np.float64) - 127.0), 8, axis=1)[..., None]
    return vals.transpose(0, 1, 3, 2).reshape(g * 512, n)
def pack4(w):
    words, scales = pack_weight(w, "e2m1")
    return words.reshape(words.shape[0], 128, -1), scales


def unpack4(words, scales):
    return unpack_weight(words.reshape(words.shape[0], 128, -1, 2), scales, "e2m1")


NB, P, Q, O, R = 4, 1024, 1024, 512, 512


def setup_inputs():
    s = mx_kscale(Q)
    t = mx_kscale(P)
    x = np.random.standard_normal((NB * P, Q)) * s
    b = np.random.standard_normal((Q, O)) / np.sqrt(Q) / s[:, None]
    x_words, x_scales = pack4(x.T)
    b_words, b_scales = pack4(b)
    return {"x_words": x_words, "x_scales": x_scales,
            "b_words": b_words, "b_scales": b_scales,
            "e": bf(0.3 * np.random.standard_normal(O)),
            "d": bf((1 + 0.1 * np.random.standard_normal((P, O))) * t[:, None]),
            "a": bf(np.random.standard_normal((P, R)) / np.sqrt(P) / t[:, None]),
            "c": bf(0.3 * np.random.standard_normal((R, O)))}


def reference(x_words, x_scales, b_words, b_scales, e, d, a, c):
    x = unpack4(x_words, x_scales)
    b = unpack4(b_words, b_scales)
    h = (x.T @ b).reshape(NB, P, O)
    z = (h + f64(e)) * f64(d)
    zq = mxq(z, 1, "e4m3")
    aq = mxq(f64(a), 0, "e4m3")
    y = aq.T @ zq.transpose(1, 0, 2).reshape(P, NB * O)
    return y.reshape(R, NB, O).transpose(1, 0, 2) + f64(c)

@@ -1,0 +1,292 @@
+from contextlib import ExitStack
+
+import concourse.mybir as mybir
+from concourse.masks import make_identity
+
+NB, NI, NJ, NO, NR = 4, 1024, 1024, 512, 512
+FLOPS = 2 * NB * NI * NJ * NO + 2 * NB * NI * NR * NO
+
+F32 = mybir.dt.float32
+BF16 = mybir.dt.bfloat16
+I32 = mybir.dt.int32
+U32 = mybir.dt.uint32
+U8 = mybir.dt.uint8
+FP4X4 = mybir.dt.float4_e2m1fn_x4
+FP8X4 = mybir.dt.float8_e4m3fn_x4
+ADD = mybir.AluOpType.add
+MULT = mybir.AluOpType.mult
+
+P = 128
+PASS = 512
+BANKS = 8
+HALF = 256
+LAST = 2 * NB - 1
+
+
+def tile_kronecker_factored_linear_s4_kernel(tc, x_words, x_scales, b_words, b_scales, e, d, a, c, out):
+    nc = tc.nc
+    with ExitStack() as ctx:
+        sb = ctx.enter_context(tc.tile_pool(name="sb", bufs=1))
+        ps = ctx.enter_context(tc.psum_pool(name="ps", bufs=1))
+        ctx.enter_context(tc.manual_schedule())
+
+        taken = []
+
+        def next_bank(shape, dtype):
+            n = len(taken)
+            taken.append(n)
+            return ps.tile(shape, dtype, name="bank_use%d" % n, tag="bank%d" % (n % BANKS))
+
+        def keep(name, shape, dtype):
+            return sb.tile(shape, dtype, name=name, tag=name, align_bytes=64)
+
+        def zero(tile):
+            nc.vector.memset(tile[:].rearrange("p g n -> p (g n)").bitcast(I32), 0)
+
+        def load_scale_rows(queue, plane, scales, r, col0, width):
+            rows = scales.rearrange("g (q r) n -> r q g n", r=4)
+            queue.dma_start(out=plane[r:P:32, :, :].bitcast(I32), in_=rows[r, :, :, col0:col0 + width].bitcast(I32))
+
+        def load_words(name, words, byte0, nbytes):
+            t = keep(name, [P, 2, nbytes], U8)
+            nc.sync.dma_start(out=t[:].bitcast(I32), in_=words.rearrange("g p n -> p g n")[:, :, byte0:byte0 + nbytes].bitcast(I32))
+            return t
+
+        def load_d(g, h):
+            t = keep("d_rows%d%d" % (g, h), [P, 2, NO], BF16)
+            i0 = g * PASS + h * HALF
+            nc.sync.dma_start(out=t[:], in_=d[i0:i0 + HALF, :].rearrange("(p u) o -> p u o", u=2))
+            return t
+
+        def load_a(g):
+            t = keep("a_rows%d" % g, [P, 4, NR], BF16)
+            nc.sync.dma_start(out=t[:], in_=a[g * PASS:(g + 1) * PASS, :].rearrange("(p j) r -> p j r", j=4))
+            return t
+
+        b_plane = keep("b_plane", [P, 2, NO], U8)
+        x_plane_first = keep("x_plane_first", [P, 2, NI], U8)
+        x_plane_rest = keep("x_plane_rest", [P, 2, (NB - 1) * NI], U8)
+        e_rows = keep("e_rows", [P, P], BF16)
+        ident_bf = keep("ident_bf", [P, P], BF16)
+        ident_f32 = keep("ident_f32", [P, P], F32)
+        nc.vector.memset(e_rows[:], 0.0)
+        zero(b_plane)
+        zero(x_plane_first)
+        zero(x_plane_rest)
+        make_identity(nc, ident_bf[:])
+        make_identity(nc, ident_f32[:])
+
+        d_rows = {}
+        x_codes = {}
+        d_rows[0, 0] = load_d(0, 0)
+        nc.sync.dma_start(out=e_rows[0:4, :], in_=e.rearrange("(c p) -> c p", p=P))
+        for r in range(4):
+            load_scale_rows(nc.sync, b_plane, b_scales, r, 0, NO)
+        d_rows[0, 1] = load_d(0, 1)
+        for r in range(4):
+            load_scale_rows(nc.sync, x_plane_first, x_scales, r, 0, NI)
+        b_codes = load_words("b_codes", b_words, 0, 2 * NO)
+        x_codes[0, 0] = load_words("x_codes00", x_words, 0, 2 * PASS)
+        x_codes[0, 1] = load_words("x_codes01", x_words, 2 * PASS, 2 * PASS)
+        a_rows = [load_a(0)]
+        d_rows[1, 0] = load_d(1, 0)
+        d_rows[1, 1] = load_d(1, 1)
+        a_rows.append(load_a(1))
+        for r in range(4):
+            load_scale_rows(nc.sync, x_plane_rest, x_scales, r, NI, (NB - 1) * NI)
+        x_sample = {1: load_words("x_codes1", x_words, 2 * NI, 2 * NI)}
+        c_sb = keep("c_sb", [P, 4, NO], BF16)
+        nc.sync.dma_start(out=c_sb[:], in_=c.rearrange("(t p) o -> p t o", p=P))
+        for m in range(2, NB):
+            x_sample[m] = load_words("x_codes%d" % m, x_words, 2 * NI * m, 2 * NI)
+
+        def x_operand(m, g, kg):
+            if m == 0:
+                return x_codes[0, g][:, kg, :], x_plane_first[:, kg, g * PASS:(g + 1) * PASS]
+            col = (m - 1) * NI + g * PASS
+            return x_sample[m][:, kg, 2 * PASS * g:2 * PASS * (g + 1)], x_plane_rest[:, kg, col:col + PASS]
+
+        e_col = keep("e_col", [P, 4], F32)
+        d_t = [keep("d_t%d" % g, [P, 4, 2, HALF], BF16) for g in range(2)]
+
+        def turn_e():
+            bank = next_bank([P, P], BF16)
+            nc.tensor.transpose(bank[:], e_rows[:], ident_bf[:])
+            nc.scalar.copy(out=e_col[:], in_=bank[:, 0:4])
+
+        def turn_d(g, h):
+            bank = next_bank([P, 4, 2, P], BF16)
+            for ot in range(4):
+                for u in range(2):
+                    nc.tensor.transpose(bank[:, ot, u, :], d_rows[g, h][:, u, P * ot:P * (ot + 1)], ident_bf[:])
+            nc.scalar.copy(out=d_t[g][:, :, :, P * h:P * (h + 1)], in_=bank[:])
+
+        h_banks = {}
+        z_t = {}
+
+        def first_product(m, g, oh, cc):
+            ot = 2 * oh + cc
+            bank = next_bank([P, PASS], F32)
+            for kg in range(2):
+                codes, plane = x_operand(m, g, kg)
+                nc.tensor.matmul_mx(
+                    out=bank[:],
+                    lhsT=b_codes[:, kg, 2 * P * ot:2 * P * (ot + 1)].bitcast(FP4X4),
+                    lhsT_scale=b_plane[:, kg, P * ot:P * (ot + 1)],
+                    rhs=codes.bitcast(FP4X4),
+                    rhs_scale=plane,
+                    start=(kg == 0),
+                    stop=(kg == 1),
+                )
+            h_banks[m, g, oh, cc] = bank
+
+        def bias_and_gain(m, g, oh, cc):
+            ot = 2 * oh + cc
+            t = keep("z_t%d%d%d" % (m, g, ot), [P, PASS], BF16)
+            nc.vector.scalar_tensor_tensor(
+                out=t[:].rearrange("p (u n) -> p u n", u=2),
+                in0=h_banks[m, g, oh, cc][:].rearrange("p (n u) -> p u n", u=2),
+                scalar=e_col[:, ot:ot + 1],
+                in1=d_t[g][:, ot, :, :],
+                op0=ADD,
+                op1=MULT,
+            )
+            z_t[m, g, oh, cc] = t
+
+        def granules(s):
+            m, k = divmod(s, 2)
+            if m == 0:
+                return [(0, k, 0), (0, k, 1)]
+            return [(m, 0, k), (m, 1, k)]
+
+        z_grouped = {}
+        z_mx = {}
+
+        def turn_z(s):
+            if s == LAST:
+                parts = [keep("z_grouped%d%d" % (s, q), [P, 4 * HALF], BF16)[:] for q in range(2)]
+                z_grouped[s, 0], z_grouped[s, 1] = parts
+            else:
+                grouped = keep("z_grouped%d" % s, [P, 8 * HALF], BF16)
+                parts = [grouped[:, 4 * HALF * q:4 * HALF * (q + 1)] for q in range(2)]
+                z_grouped[s, 0] = grouped[:]
+            for q, (m, g, oh) in enumerate(granules(s)):
+                bank = next_bank([P, 2, 2, P], F32)
+                for cc in range(2):
+                    words = z_t[m, g, oh, cc][:].bitcast(F32)
+                    for u in range(2):
+                        nc.tensor.transpose(bank[:, cc, u, :], words[:, P * u:P * (u + 1)], ident_f32[:])
+                nc.scalar.copy(
+                    out=parts[q].bitcast(F32).rearrange("p (cc o u) -> p cc o u", cc=2, u=2),
+                    in_=bank[:].rearrange("p cc u o -> p cc o u"),
+                )
+
+        def quantize_z(s, qs=(0, 1)):
+            width = HALF * len(qs)
+            codes = keep("z_codes%d%d" % (s, qs[0]), [P, width], U32)
+            plane = keep("z_plane%d%d" % (s, qs[0]), [P, width], U8)
+            nc.vector.quantize_mx(out=codes[:].bitcast(FP8X4), scales=plane[:], in_=z_grouped[s, qs[0]])
+            for n, q in enumerate(qs):
+                z_mx[granules(s)[q]] = (codes[:, HALF * n:HALF * (n + 1)], plane[:, HALF * n:HALF * (n + 1)])
+
+        a_grouped = [keep("a_grouped%d" % g, [P, NR * 4], BF16) for g in range(2)]
+        a_mx = {}
+
+        def group_a(g, half):
+            cols = slice(HALF * half, HALF * (half + 1))
+            nc.scalar.copy(
+                out=a_grouped[g][:, 4 * HALF * half:4 * HALF * (half + 1)].rearrange("p (k i u e) -> p k u e i", i=4, u=2, e=2),
+                in_=a_rows[g][:, :, cols].rearrange("p (e u) (k i) -> p k u e i", u=2, i=4),
+            )
+
+        def quantize_a(g):
+            codes = keep("a_codes%d" % g, [P, NR], U32)
+            plane = keep("a_plane%d" % g, [P, NR], U8)
+            nc.vector.quantize_mx(out=codes[:].bitcast(FP8X4), scales=plane[:], in_=a_grouped[g][:])
+            a_mx[g] = (codes, plane)
+
+        y_banks = {}
+
+        def second_product(k, rp):
+            m, oh = divmod(k, 2)
+            bank = next_bank([P, 2, HALF], F32)
+            for rr in range(2):
+                r0 = P * (2 * rp + rr)
+                for g in range(2):
+                    nc.tensor.matmul_mx(
+                        out=bank[:, rr, :],
+                        lhsT=a_mx[g][0][:, r0:r0 + P].bitcast(FP8X4),
+                        lhsT_scale=a_mx[g][1][:, r0:r0 + P],
+                        rhs=z_mx[m, g, oh][0].bitcast(FP8X4),
+                        rhs_scale=z_mx[m, g, oh][1],
+                        start=(g == 0),
+                        stop=(g == 1),
+                    )
+            y_banks[k, rp] = bank
+
+        def add_and_store(k, rp):
+            m, oh = divmod(k, 2)
+            y = keep("y%d%d" % (k, rp), [P, 2, HALF], F32)
+            nc.vector.tensor_tensor(out=y[:], in0=y_banks[k, rp][:], in1=c_sb[:, 2 * rp:2 * rp + 2, HALF * oh:HALF * (oh + 1)], op=ADD)
+            nc.sync.dma_start(
+                out=out[m, HALF * rp:HALF * (rp + 1), HALF * oh:HALF * (oh + 1)].rearrange("(t p) o -> p t o", p=P),
+                in_=y[:],
+            )
+
+        def finish(k):
+            for rp in range(2):
+                second_product(k, rp)
+                add_and_store(k, rp)
+
+        def tiles(s):
+            return [(m, g, oh, cc) for (m, g, oh) in granules(s) for cc in range(2)]
+
+        def stage_one(s):
+            for key in tiles(s):
+                first_product(*key)
+                bias_and_gain(*key)
+
+        turn_d(0, 0)
+        turn_e()
+        turn_d(0, 1)
+        stage_one(0)
+        group_a(0, 0)
+        group_a(0, 1)
+        turn_d(1, 0)
+        turn_d(1, 1)
+        stage_one(1)
+        quantize_a(0)
+        group_a(1, 0)
+        group_a(1, 1)
+        turn_z(0)
+        stage_one(2)
+        quantize_a(1)
+        quantize_z(0)
+        turn_z(1)
+        for n, key in enumerate(tiles(3)):
+            first_product(*key)
+            bias_and_gain(*key)
+            if n == 1:
+                quantize_z(1)
+        turn_z(2)
+        finish(0)
+        finish(1)
+        for s in range(4, LAST + 1):
+            quantize_z(s - 2)
+            stage_one(s)
+            turn_z(s - 1)
+            if s < LAST:
+                finish(s - 2)
+        second_product(LAST - 2, 0)
+        second_product(LAST - 2, 1)
+        quantize_z(LAST - 1)
+        add_and_store(LAST - 2, 0)
+        add_and_store(LAST - 2, 1)
+        turn_z(LAST)
+        second_product(LAST - 1, 0)
+        second_product(LAST - 1, 1)
+        quantize_z(LAST, (0,))
+        quantize_z(LAST, (1,))
+        add_and_store(LAST - 1, 0)
+        add_and_store(LAST - 1, 1)
+        finish(LAST)

@@ -21,6 +21,7 @@ PASS = 512
 BANKS = 8
 HALF = 256
 LAST = 2 * NB - 1
+ON_GPSIMD = {(k, 2) for k in range(5)}
 
 
 def tile_kronecker_factored_linear_s4_kernel(tc, x_words, x_scales, b_words, b_scales, e, d, a, c, out):
@@ -65,13 +66,15 @@ def tile_kronecker_factored_linear_s4_kernel(tc, x_words, x_scales, b_words, b_s
 
         b_plane = keep("b_plane", [P, 2, NO], U8)
         x_plane_first = keep("x_plane_first", [P, 2, NI], U8)
-        x_plane_rest = keep("x_plane_rest", [P, 2, (NB - 1) * NI], U8)
+        x_plane_second = keep("x_plane_second", [P, 2, NI], U8)
+        x_plane_rest = keep("x_plane_rest", [P, 2, (NB - 2) * NI], U8)
         e_rows = keep("e_rows", [P, P], BF16)
         ident_bf = keep("ident_bf", [P, P], BF16)
         ident_f32 = keep("ident_f32", [P, P], F32)
         nc.vector.memset(e_rows[:], 0.0)
         zero(b_plane)
         zero(x_plane_first)
+        zero(x_plane_second)
         zero(x_plane_rest)
         make_identity(nc, ident_bf[:])
         make_identity(nc, ident_f32[:])
@@ -91,20 +94,26 @@ def tile_kronecker_factored_linear_s4_kernel(tc, x_words, x_scales, b_words, b_s
         a_rows = [load_a(0)]
         d_rows[1, 0] = load_d(1, 0)
         d_rows[1, 1] = load_d(1, 1)
-        a_rows.append(load_a(1))
         for r in range(4):
-            load_scale_rows(nc.sync, x_plane_rest, x_scales, r, NI, (NB - 1) * NI)
+            load_scale_rows(nc.sync, x_plane_second, x_scales, r, NI, NI)
         x_sample = {1: load_words("x_codes1", x_words, 2 * NI, 2 * NI)}
+        a_rows.append(load_a(1))
         c_sb = keep("c_sb", [P, 4, NO], BF16)
         nc.sync.dma_start(out=c_sb[:], in_=c.rearrange("(t p) o -> p t o", p=P))
+        for r in range(4):
+            load_scale_rows(nc.sync, x_plane_rest, x_scales, r, 2 * NI, (NB - 2) * NI)
         for m in range(2, NB):
             x_sample[m] = load_words("x_codes%d" % m, x_words, 2 * NI * m, 2 * NI)
 
         def x_operand(m, g, kg):
             if m == 0:
                 return x_codes[0, g][:, kg, :], x_plane_first[:, kg, g * PASS:(g + 1) * PASS]
-            col = (m - 1) * NI + g * PASS
-            return x_sample[m][:, kg, 2 * PASS * g:2 * PASS * (g + 1)], x_plane_rest[:, kg, col:col + PASS]
+            if m == 1:
+                plane = x_plane_second[:, kg, g * PASS:(g + 1) * PASS]
+            else:
+                col = (m - 2) * NI + g * PASS
+                plane = x_plane_rest[:, kg, col:col + PASS]
+            return x_sample[m][:, kg, 2 * PASS * g:2 * PASS * (g + 1)], plane
 
         e_col = keep("e_col", [P, 4], F32)
         d_t = [keep("d_t%d" % g, [P, 4, 2, HALF], BF16) for g in range(2)]
@@ -207,11 +216,11 @@ def tile_kronecker_factored_linear_s4_kernel(tc, x_words, x_scales, b_words, b_s
 
         y_banks = {}
 
-        def second_product(k, rp):
+        def second_product(k, rt0, count=2):
             m, oh = divmod(k, 2)
-            bank = next_bank([P, 2, HALF], F32)
-            for rr in range(2):
-                r0 = P * (2 * rp + rr)
+            bank = next_bank([P, count, HALF], F32)
+            for rr in range(count):
+                r0 = P * (rt0 + rr)
                 for g in range(2):
                     nc.tensor.matmul_mx(
                         out=bank[:, rr, :],
@@ -222,71 +231,89 @@ def tile_kronecker_factored_linear_s4_kernel(tc, x_words, x_scales, b_words, b_s
                         start=(g == 0),
                         stop=(g == 1),
                     )
-            y_banks[k, rp] = bank
+            y_banks[k, rt0] = bank
 
-        def add_and_store(k, rp):
+        def add_and_store(k, rt0, count=2):
             m, oh = divmod(k, 2)
-            y = keep("y%d%d" % (k, rp), [P, 2, HALF], F32)
-            nc.vector.tensor_tensor(out=y[:], in0=y_banks[k, rp][:], in1=c_sb[:, 2 * rp:2 * rp + 2, HALF * oh:HALF * (oh + 1)], op=ADD)
+            y = keep("y%d%d" % (k, rt0), [P, count, HALF], F32)
+            c_part = c_sb[:, rt0:rt0 + count, HALF * oh:HALF * (oh + 1)]
+            if (k, rt0) in ON_GPSIMD:
+                sums = keep("sums%d%d" % (k, rt0), [P, count, HALF], F32)
+                nc.scalar.copy(out=sums[:], in_=y_banks[k, rt0][:])
+                nc.gpsimd.tensor_tensor(out=y[:], in0=sums[:], in1=c_part, op=ADD)
+            else:
+                nc.vector.tensor_tensor(out=y[:], in0=y_banks[k, rt0][:], in1=c_part, op=ADD)
             nc.sync.dma_start(
-                out=out[m, HALF * rp:HALF * (rp + 1), HALF * oh:HALF * (oh + 1)].rearrange("(t p) o -> p t o", p=P),
+                out=out[m, P * rt0:P * (rt0 + count), HALF * oh:HALF * (oh + 1)].rearrange("(t p) o -> p t o", p=P),
                 in_=y[:],
             )
 
-        def finish(k):
-            for rp in range(2):
-                second_product(k, rp)
-                add_and_store(k, rp)
+        def finish(k, pieces=((0, 2), (2, 2))):
+            for rt0, count in pieces:
+                second_product(k, rt0, count)
+                add_and_store(k, rt0, count)
 
         def tiles(s):
             return [(m, g, oh, cc) for (m, g, oh) in granules(s) for cc in range(2)]
 
-        def stage_one(s):
-            for key in tiles(s):
-                first_product(*key)
-                bias_and_gain(*key)
+        def first_stage(key):
+            first_product(*key)
+            bias_and_gain(*key)
 
         turn_d(0, 0)
         turn_e()
         turn_d(0, 1)
-        stage_one(0)
+        for key in tiles(0):
+            first_stage(key)
         group_a(0, 0)
         group_a(0, 1)
         turn_d(1, 0)
         turn_d(1, 1)
-        stage_one(1)
         quantize_a(0)
+        for key in tiles(1):
+            first_stage(key)
+        turn_z(0)
         group_a(1, 0)
         group_a(1, 1)
-        turn_z(0)
-        stage_one(2)
-        quantize_a(1)
+        for key in tiles(2):
+            first_stage(key)
         quantize_z(0)
+        quantize_a(1)
         turn_z(1)
         for n, key in enumerate(tiles(3)):
-            first_product(*key)
-            bias_and_gain(*key)
+            first_stage(key)
             if n == 1:
                 quantize_z(1)
         turn_z(2)
         finish(0)
         finish(1)
+        quantize_z(2)
         for s in range(4, LAST + 1):
-            quantize_z(s - 2)
-            stage_one(s)
-            turn_z(s - 1)
-            if s < LAST:
+            keys = tiles(s)
+            if s < 4:
+                for key in keys:
+                    first_stage(key)
+                turn_z(s - 1)
                 finish(s - 2)
-        second_product(LAST - 2, 0)
-        second_product(LAST - 2, 1)
-        quantize_z(LAST - 1)
-        add_and_store(LAST - 2, 0)
-        add_and_store(LAST - 2, 1)
+                quantize_z(s - 1)
+            else:
+                first_stage(keys[0])
+                first_stage(keys[1])
+                turn_z(s - 1)
+                first_stage(keys[2])
+                if 0 == 0:
+                    quantize_z(s - 1)
+                first_stage(keys[3])
+                if 0 == 1:
+                    quantize_z(s - 1)
+                finish(s - 2)
+                if 0 == 2:
+                    quantize_z(s - 1)
         turn_z(LAST)
         second_product(LAST - 1, 0)
-        second_product(LAST - 1, 1)
+        second_product(LAST - 1, 2)
         quantize_z(LAST, (0,))
         quantize_z(LAST, (1,))
         add_and_store(LAST - 1, 0)
-        add_and_store(LAST - 1, 1)
-        finish(LAST)
+        add_and_store(LAST - 1, 2)
+        finish(LAST, ((0, 2), (2, 1), (3, 1)))

from contextlib import ExitStack

import concourse.mybir as mybir
from concourse.masks import make_identity

NB, NI, NJ, NO, NR = 4, 1024, 1024, 512, 512
FLOPS = 2 * NB * NI * NJ * NO + 2 * NB * NI * NR * NO

F32 = mybir.dt.float32
BF16 = mybir.dt.bfloat16
I32 = mybir.dt.int32
U32 = mybir.dt.uint32
U8 = mybir.dt.uint8
FP4X4 = mybir.dt.float4_e2m1fn_x4
FP8X4 = mybir.dt.float8_e4m3fn_x4
ADD = mybir.AluOpType.add
MULT = mybir.AluOpType.mult

P = 128
PASS = 512
BANKS = 8
HALF = 256
LAST = 2 * NB - 1
ON_GPSIMD = {(k, 2) for k in range(5)}


def tile_kronecker_factored_linear_s4_kernel(tc, x_words, x_scales, b_words, b_scales, e, d, a, c, out):
    nc = tc.nc
    with ExitStack() as ctx:
        sb = ctx.enter_context(tc.tile_pool(name="sb", bufs=1))
        ps = ctx.enter_context(tc.psum_pool(name="ps", bufs=1))
        ctx.enter_context(tc.manual_schedule())

        taken = []

        def next_bank(shape, dtype):
            n = len(taken)
            taken.append(n)
            return ps.tile(shape, dtype, name="bank_use%d" % n, tag="bank%d" % (n % BANKS))

        def keep(name, shape, dtype):
            return sb.tile(shape, dtype, name=name, tag=name, align_bytes=64)

        def zero(tile):
            nc.vector.memset(tile[:].rearrange("p g n -> p (g n)").bitcast(I32), 0)

        def load_scale_rows(queue, plane, scales, r, col0, width):
            rows = scales.rearrange("g (q r) n -> r q g n", r=4)
            queue.dma_start(out=plane[r:P:32, :, :].bitcast(I32), in_=rows[r, :, :, col0:col0 + width].bitcast(I32))

        def load_words(name, words, byte0, nbytes):
            t = keep(name, [P, 2, nbytes], U8)
            nc.sync.dma_start(out=t[:].bitcast(I32), in_=words.rearrange("g p n -> p g n")[:, :, byte0:byte0 + nbytes].bitcast(I32))
            return t

        def load_d(g, h):
            t = keep("d_rows%d%d" % (g, h), [P, 2, NO], BF16)
            i0 = g * PASS + h * HALF
            nc.sync.dma_start(out=t[:], in_=d[i0:i0 + HALF, :].rearrange("(p u) o -> p u o", u=2))
            return t

        def load_a(g):
            t = keep("a_rows%d" % g, [P, 4, NR], BF16)
            nc.sync.dma_start(out=t[:], in_=a[g * PASS:(g + 1) * PASS, :].rearrange("(p j) r -> p j r", j=4))
            return t

        b_plane = keep("b_plane", [P, 2, NO], U8)
        x_plane_first = keep("x_plane_first", [P, 2, NI], U8)
        x_plane_second = keep("x_plane_second", [P, 2, NI], U8)
        x_plane_rest = keep("x_plane_rest", [P, 2, (NB - 2) * NI], U8)
        e_rows = keep("e_rows", [P, P], BF16)
        ident_bf = keep("ident_bf", [P, P], BF16)
        ident_f32 = keep("ident_f32", [P, P], F32)
        nc.vector.memset(e_rows[:], 0.0)
        zero(b_plane)
        zero(x_plane_first)
        zero(x_plane_second)
        zero(x_plane_rest)
        make_identity(nc, ident_bf[:])
        make_identity(nc, ident_f32[:])

        d_rows = {}
        x_codes = {}
        d_rows[0, 0] = load_d(0, 0)
        nc.sync.dma_start(out=e_rows[0:4, :], in_=e.rearrange("(c p) -> c p", p=P))
        for r in range(4):
            load_scale_rows(nc.sync, b_plane, b_scales, r, 0, NO)
        d_rows[0, 1] = load_d(0, 1)
        for r in range(4):
            load_scale_rows(nc.sync, x_plane_first, x_scales, r, 0, NI)
        b_codes = load_words("b_codes", b_words, 0, 2 * NO)
        x_codes[0, 0] = load_words("x_codes00", x_words, 0, 2 * PASS)
        x_codes[0, 1] = load_words("x_codes01", x_words, 2 * PASS, 2 * PASS)
        a_rows = [load_a(0)]
        d_rows[1, 0] = load_d(1, 0)
        d_rows[1, 1] = load_d(1, 1)
        for r in range(4):
            load_scale_rows(nc.sync, x_plane_second, x_scales, r, NI, NI)
        x_sample = {1: load_words("x_codes1", x_words, 2 * NI, 2 * NI)}
        a_rows.append(load_a(1))
        c_sb = keep("c_sb", [P, 4, NO], BF16)
        nc.sync.dma_start(out=c_sb[:], in_=c.rearrange("(t p) o -> p t o", p=P))
        for r in range(4):
            load_scale_rows(nc.sync, x_plane_rest, x_scales, r, 2 * NI, (NB - 2) * NI)
        for m in range(2, NB):
            x_sample[m] = load_words("x_codes%d" % m, x_words, 2 * NI * m, 2 * NI)

        def x_operand(m, g, kg):
            if m == 0:
                return x_codes[0, g][:, kg, :], x_plane_first[:, kg, g * PASS:(g + 1) * PASS]
            if m == 1:
                plane = x_plane_second[:, kg, g * PASS:(g + 1) * PASS]
            else:
                col = (m - 2) * NI + g * PASS
                plane = x_plane_rest[:, kg, col:col + PASS]
            return x_sample[m][:, kg, 2 * PASS * g:2 * PASS * (g + 1)], plane

        e_col = keep("e_col", [P, 4], F32)
        d_t = [keep("d_t%d" % g, [P, 4, 2, HALF], BF16) for g in range(2)]

        def turn_e():
            bank = next_bank([P, P], BF16)
            nc.tensor.transpose(bank[:], e_rows[:], ident_bf[:])
            nc.scalar.copy(out=e_col[:], in_=bank[:, 0:4])

        def turn_d(g, h):
            bank = next_bank([P, 4, 2, P], BF16)
            for ot in range(4):
                for u in range(2):
                    nc.tensor.transpose(bank[:, ot, u, :], d_rows[g, h][:, u, P * ot:P * (ot + 1)], ident_bf[:])
            nc.scalar.copy(out=d_t[g][:, :, :, P * h:P * (h + 1)], in_=bank[:])

        h_banks = {}
        z_t = {}

        def first_product(m, g, oh, cc):
            ot = 2 * oh + cc
            bank = next_bank([P, PASS], F32)
            for kg in range(2):
                codes, plane = x_operand(m, g, kg)
                nc.tensor.matmul_mx(
                    out=bank[:],
                    lhsT=b_codes[:, kg, 2 * P * ot:2 * P * (ot + 1)].bitcast(FP4X4),
                    lhsT_scale=b_plane[:, kg, P * ot:P * (ot + 1)],
                    rhs=codes.bitcast(FP4X4),
                    rhs_scale=plane,
                    start=(kg == 0),
                    stop=(kg == 1),
                )
            h_banks[m, g, oh, cc] = bank

        def bias_and_gain(m, g, oh, cc):
            ot = 2 * oh + cc
            t = keep("z_t%d%d%d" % (m, g, ot), [P, PASS], BF16)
            nc.vector.scalar_tensor_tensor(
                out=t[:].rearrange("p (u n) -> p u n", u=2),
                in0=h_banks[m, g, oh, cc][:].rearrange("p (n u) -> p u n", u=2),
                scalar=e_col[:, ot:ot + 1],
                in1=d_t[g][:, ot, :, :],
                op0=ADD,
                op1=MULT,
            )
            z_t[m, g, oh, cc] = t

        def granules(s):
            m, k = divmod(s, 2)
            if m == 0:
                return [(0, k, 0), (0, k, 1)]
            return [(m, 0, k), (m, 1, k)]

        z_grouped = {}
        z_mx = {}

        def turn_z(s):
            if s == LAST:
                parts = [keep("z_grouped%d%d" % (s, q), [P, 4 * HALF], BF16)[:] for q in range(2)]
                z_grouped[s, 0], z_grouped[s, 1] = parts
            else:
                grouped = keep("z_grouped%d" % s, [P, 8 * HALF], BF16)
                parts = [grouped[:, 4 * HALF * q:4 * HALF * (q + 1)] for q in range(2)]
                z_grouped[s, 0] = grouped[:]
            for q, (m, g, oh) in enumerate(granules(s)):
                bank = next_bank([P, 2, 2, P], F32)
                for cc in range(2):
                    words = z_t[m, g, oh, cc][:].bitcast(F32)
                    for u in range(2):
                        nc.tensor.transpose(bank[:, cc, u, :], words[:, P * u:P * (u + 1)], ident_f32[:])
                nc.scalar.copy(
                    out=parts[q].bitcast(F32).rearrange("p (cc o u) -> p cc o u", cc=2, u=2),
                    in_=bank[:].rearrange("p cc u o -> p cc o u"),
                )

        def quantize_z(s, qs=(0, 1)):
            width = HALF * len(qs)
            codes = keep("z_codes%d%d" % (s, qs[0]), [P, width], U32)
            plane = keep("z_plane%d%d" % (s, qs[0]), [P, width], U8)
            nc.vector.quantize_mx(out=codes[:].bitcast(FP8X4), scales=plane[:], in_=z_grouped[s, qs[0]])
            for n, q in enumerate(qs):
                z_mx[granules(s)[q]] = (codes[:, HALF * n:HALF * (n + 1)], plane[:, HALF * n:HALF * (n + 1)])

        a_grouped = [keep("a_grouped%d" % g, [P, NR * 4], BF16) for g in range(2)]
        a_mx = {}

        def group_a(g, half):
            cols = slice(HALF * half, HALF * (half + 1))
            nc.scalar.copy(
                out=a_grouped[g][:, 4 * HALF * half:4 * HALF * (half + 1)].rearrange("p (k i u e) -> p k u e i", i=4, u=2, e=2),
                in_=a_rows[g][:, :, cols].rearrange("p (e u) (k i) -> p k u e i", u=2, i=4),
            )

        def quantize_a(g):
            codes = keep("a_codes%d" % g, [P, NR], U32)
            plane = keep("a_plane%d" % g, [P, NR], U8)
            nc.vector.quantize_mx(out=codes[:].bitcast(FP8X4), scales=plane[:], in_=a_grouped[g][:])
            a_mx[g] = (codes, plane)

        y_banks = {}

        def second_product(k, rt0, count=2):
            m, oh = divmod(k, 2)
            bank = next_bank([P, count, HALF], F32)
            for rr in range(count):
                r0 = P * (rt0 + rr)
                for g in range(2):
                    nc.tensor.matmul_mx(
                        out=bank[:, rr, :],
                        lhsT=a_mx[g][0][:, r0:r0 + P].bitcast(FP8X4),
                        lhsT_scale=a_mx[g][1][:, r0:r0 + P],
                        rhs=z_mx[m, g, oh][0].bitcast(FP8X4),
                        rhs_scale=z_mx[m, g, oh][1],
                        start=(g == 0),
                        stop=(g == 1),
                    )
            y_banks[k, rt0] = bank

        def add_and_store(k, rt0, count=2):
            m, oh = divmod(k, 2)
            y = keep("y%d%d" % (k, rt0), [P, count, HALF], F32)
            c_part = c_sb[:, rt0:rt0 + count, HALF * oh:HALF * (oh + 1)]
            if (k, rt0) in ON_GPSIMD:
                sums = keep("sums%d%d" % (k, rt0), [P, count, HALF], F32)
                nc.scalar.copy(out=sums[:], in_=y_banks[k, rt0][:])
                nc.gpsimd.tensor_tensor(out=y[:], in0=sums[:], in1=c_part, op=ADD)
            else:
                nc.vector.tensor_tensor(out=y[:], in0=y_banks[k, rt0][:], in1=c_part, op=ADD)
            nc.sync.dma_start(
                out=out[m, P * rt0:P * (rt0 + count), HALF * oh:HALF * (oh + 1)].rearrange("(t p) o -> p t o", p=P),
                in_=y[:],
            )

        def finish(k, pieces=((0, 2), (2, 2))):
            for rt0, count in pieces:
                second_product(k, rt0, count)
                add_and_store(k, rt0, count)

        def tiles(s):
            return [(m, g, oh, cc) for (m, g, oh) in granules(s) for cc in range(2)]

        def first_stage(key):
            first_product(*key)
            bias_and_gain(*key)

        turn_d(0, 0)
        turn_e()
        turn_d(0, 1)
        for key in tiles(0):
            first_stage(key)
        group_a(0, 0)
        group_a(0, 1)
        turn_d(1, 0)
        turn_d(1, 1)
        quantize_a(0)
        for key in tiles(1):
            first_stage(key)
        turn_z(0)
        group_a(1, 0)
        group_a(1, 1)
        for key in tiles(2):
            first_stage(key)
        quantize_z(0)
        quantize_a(1)
        turn_z(1)
        for n, key in enumerate(tiles(3)):
            first_stage(key)
            if n == 1:
                quantize_z(1)
        turn_z(2)
        finish(0)
        finish(1)
        quantize_z(2)
        for s in range(4, LAST + 1):
            keys = tiles(s)
            if s < 4:
                for key in keys:
                    first_stage(key)
                turn_z(s - 1)
                finish(s - 2)
                quantize_z(s - 1)
            else:
                first_stage(keys[0])
                first_stage(keys[1])
                turn_z(s - 1)
                first_stage(keys[2])
                if 0 == 0:
                    quantize_z(s - 1)
                first_stage(keys[3])
                if 0 == 1:
                    quantize_z(s - 1)
                finish(s - 2)
                if 0 == 2:
                    quantize_z(s - 1)
        turn_z(LAST)
        second_product(LAST - 1, 0)
        second_product(LAST - 1, 2)
        quantize_z(LAST, (0,))
        quantize_z(LAST, (1,))
        add_and_store(LAST - 1, 0)
        add_and_store(LAST - 1, 2)
        finish(LAST, ((0, 2), (2, 1), (3, 1)))
